import numpy as np
import ml_dtypes


def mxq(x, axis, fmt="e4m3"):
    dtype, down = {"e4m3": (ml_dtypes.float8_e4m3fn, 7), "e5m2": (ml_dtypes.float8_e5m2, 14)}[fmt]
    v = np.moveaxis(np.asarray(x, np.float32).astype(ml_dtypes.bfloat16).astype(np.float64), axis, -1)
    blocks = v.reshape(v.shape[:-1] + (-1, 32))
    amax = np.abs(blocks).max(-1, keepdims=True)
    byte = np.maximum(np.where(amax > 0, np.frexp(amax)[1] - 1 + 127, 0) - down, 1)
    scale = np.exp2(byte - 127.0)
    codes = (blocks / scale).astype(np.float32).astype(dtype).astype(np.float64)
    return np.moveaxis((codes * scale).reshape(v.shape), -1, axis)


WIDE = False


def mx_kscale(k, group=512):
    if not WIDE:
        return np.ones(k)
    levels = np.array([10, -10, 5, -5, 0])
    if group != 512:
        return np.exp2(np.random.permutation(np.resize(levels, k // group))).repeat(group)
    if k % 512:
        return np.exp2(np.random.permutation(np.resize(levels, k // 32))).repeat(32)
    a = np.empty((k // 512, 16))
    for p in range(k // 512):
        a[p, :8] = np.random.permutation(np.resize(levels, 8))
        for g in range(8):
            far = levels[np.abs(levels - a[p, g]) >= 10]
            a[p, g + 8] = far[np.random.randint(len(far))]
    return np.exp2(a.ravel()).repeat(32)


def f64(x):
    return np.asarray(x).astype(np.float64)


E2M1 = np.array([0.0, 0.5, 1.0, 1.5, 2.0, 3.0, 4.0, 6.0, -0.0, -0.5, -1.0, -1.5, -2.0, -3.0, -4.0, -6.0])


def pack_group(w):
    k, n = w.shape
    w = f64(np.asarray(w, np.float32).astype(ml_dtypes.bfloat16)).reshape(k // 32, 32, n)
    amax = np.abs(w).max(1)
    mant, ex = np.frexp(amax / 6.0)
    byte = np.clip(np.where(amax > 0, np.where(mant > 0.5, ex, ex - 1) + 127, 1), 1, 254)
    scaled = (w * np.exp2(127.0 - byte)[:, None, :]).reshape(k, n).astype(np.float32)
    c = np.ascontiguousarray(scaled.reshape(k // 4, 4, n).transpose(0, 2, 1)).astype(ml_dtypes.float4_e2m1fn).view(np.uint8) & 0xF
    return np.ascontiguousarray((c[..., 0::2] | (c[..., 1::2] << 4)).reshape(k // 4, 2 * n)), byte.astype(np.uint8)


def unpack_group(words, scales):
    p, n = words.shape[0], scales.shape[1]
    words = np.ascontiguousarray(words).reshape(p, n, 2)
    nib = np.empty((p, n, 4), np.uint8)
    nib[..., 0::2] = words & 0xF
    nib[..., 1::2] = words >> 4
    return E2M1[nib].transpose(0, 2, 1).reshape(4 * p, n) * np.repeat(np.exp2(scales.astype(np.float64) - 127.0), 32, axis=0)


def sigmoid(v):
    return 1.0 / (1.0 + np.exp(-v))


G, D, M, O, N = 2, 256, 256, 256, 512


def setup_inputs():
    n = np.random.standard_normal
    s_d = mx_kscale(D, 0)
    s_o = mx_kscale(O, 0)
    w1_ = [pack_group(w) for w in n((G, D, M)) / np.sqrt(D) / s_d[:, None]]
    w2_ = [pack_group(w) for w in n((G, D, M)) / np.sqrt(D) / s_d[:, None]]
    wo_ = [pack_group(w) for w in n((G, O, M)) / np.sqrt(O) / s_o[:, None]]
    return {
        "x": (n((G, D, N)) * s_d[:, None]).astype(np.float32),
        "w1_words": np.stack([w[0] for w in w1_]),
        "w1_scales": np.stack([w[1] for w in w1_]),
        "w2_words": np.stack([w[0] for w in w2_]),
        "w2_scales": np.stack([w[1] for w in w2_]),
        "st": (np.random.uniform(4.0, 16.0, (G, M, 1))).astype(np.float32),
        "gb": (0.5 * n((G, M, 1))).astype(np.float32),
        "wo_words": np.stack([w[0] for w in wo_]),
        "wo_scales": np.stack([w[1] for w in wo_]),
        "dy": (n((G, O, N)) * s_o[:, None]).astype(np.float32),
        "old": (0.3 * n((G, M, N))).astype(np.float32),
    }


def reference(x, w1_words, w1_scales, w2_words, w2_scales, st, gb, wo_words, wo_scales, dy, old):
    w1 = np.stack([unpack_group(w1_words[g], w1_scales[g]) for g in range(G)])
    xq = mxq(f64(x), 1, "e4m3")
    z1 = w1.transpose(0, 2, 1) @ xq
    w2 = np.stack([unpack_group(w2_words[g], w2_scales[g]) for g in range(G)])
    z2 = w2.transpose(0, 2, 1) @ xq
    mu = np.mean(z1 * z2, axis=-1, keepdims=True)
    gt = sigmoid(mu * f64(st) + f64(gb))
    wo = np.stack([unpack_group(wo_words[g], wo_scales[g]) for g in range(G)])
    dyq = mxq(f64(dy), 1, "e4m3")
    c0 = wo.transpose(0, 2, 1) @ dyq
    dgt = np.sum(c0 * z1, axis=-1, keepdims=True)
    dmu = dgt * gt * (1.0 - gt) * f64(st)
    dz1 = c0 * gt + dmu / 512.0 * z2
    y = dz1 + f64(old)
    return y

@@ -1,0 +1,198 @@
+from contextlib import ExitStack
+
+import concourse.mybir as mybir
+
+G, D, M, N = 2, 256, 256, 512
+FLOPS = 3 * 2 * G * D * M * N
+
+F32 = mybir.dt.float32
+BF16 = mybir.dt.bfloat16
+I32 = mybir.dt.int32
+U32 = mybir.dt.uint32
+U8 = mybir.dt.uint8
+FP8X4 = mybir.dt.float8_e4m3fn_x4
+FP4X4 = mybir.dt.float4_e2m1fn_x4
+ALU = mybir.AluOpType
+ACT = mybir.ActivationFunctionType
+
+P = 128
+ROWS = 64
+HALF = N // 2
+V_COLS = 176
+TILES = [(g, h) for h in range(2) for g in range(G)]
+
+
+def tile_rows_browgate_kernel(tc, x, w1_words, w1_scales, w2_words, w2_scales, st, gb, wo_words, wo_scales, dy, old, out):
+    nc = tc.nc
+    with ExitStack() as ctx:
+        sb = ctx.enter_context(tc.tile_pool(name="sb", bufs=1))
+        ps = ctx.enter_context(tc.psum_pool(name="ps", bufs=1))
+        ctx.enter_context(tc.manual_schedule())
+
+        def tiles(name, count, shape, dtype, pool=sb):
+            if pool is sb:
+                return [pool.tile(shape, dtype, name="%s%d" % (name, i), align_bytes=64) for i in range(count)]
+            return [pool.tile(shape, dtype, name="%s%d" % (name, i)) for i in range(count)]
+
+        x_raw = tiles("x_raw", 2, [P, 4, HALF], F32)
+        dy_raw = tiles("dy_raw", 2, [P, 4, HALF], F32)
+        x_bf = tiles("x_bf", 2, [P, HALF, 4], BF16)
+        dy_bf = tiles("dy_bf", 2, [P, HALF, 4], BF16)
+        x_codes, dy_codes = tiles("codes", 2, [P, N], U32)
+        x_scales, dy_scales = tiles("scales", 2, [P, N], U8)
+        w_words = tiles("w_words", 3, [P, 2 * M], U8)
+        (w_scales,) = tiles("w_scales", 1, [P, 3 * M], U8)
+        rows, cols = tiles("consts", 2, [P, 2 * P], F32)
+        old_sb = tiles("old_sb", 4, [P, N], F32)
+        z1_sb = tiles("z1_sb", 4, [P, N], F32)
+        u_sb = tiles("u_sb", 4, [P, N], F32)
+        v_sb = tiles("v_sb", 4, [P, N], F32)
+        y_sb = tiles("y_sb", 4, [P, N], F32)
+        junk_mu = tiles("junk_mu", 4, [P, N], F32)
+        junk_dg = tiles("junk_dg", 4, [P, N], F32)
+        mu = tiles("mu", 4, [P, 1], F32)
+        gt = tiles("gt", 4, [P, 1], F32)
+        rest = tiles("rest", 4, [P, 1], F32)
+        slope = tiles("slope", 4, [P, 1], F32)
+        coef = tiles("coef", 4, [P, 1], F32)
+        bank_a = tiles("bank_a", 4, [P, N], F32, ps)
+        bank_b = tiles("bank_b", 4, [P, N], F32, ps)
+
+        def load_half(dst, src, half):
+            view = src.rearrange("g (p j) n -> (g p) j n", j=4)
+            nc.sync.dma_start(out=dst[half][:], in_=view[:, :, half * HALF : (half + 1) * HALF])
+
+        def load_words(i, words):
+            nc.sync.dma_start(out=w_words[i][:].bitcast(I32), in_=words.rearrange("g p b -> (g p) b").bitcast(I32))
+
+        def load_scales(queue, i, scales):
+            flat = scales.rearrange("g f m -> (g f) m").bitcast(I32)
+            for q in range(4):
+                queue.dma_start(out=w_scales[32 * q : 32 * q + 4, i * M : (i + 1) * M].bitcast(I32), in_=flat[4 * q : 4 * q + 4, :])
+
+        def load_const(i, vec):
+            nc.gpsimd.dma_start(
+                out=rows[0:P:32, i * P : (i + 1) * P].rearrange("a (c j) -> a c j", j=32),
+                in_=vec.rearrange("g (h a j) o -> a (g h) (j o)", a=4, j=32),
+            )
+
+        def cast(copy, dst, src, lo, hi):
+            copy(
+                out=dst[:, lo:hi, :].rearrange("p (c i) j -> p c j i", i=4),
+                in_=src[:, :, lo:hi].rearrange("p j (c i) -> p c j i", i=4),
+            )
+
+        def quantize(codes, scales, src, half):
+            span = slice(half * HALF, (half + 1) * HALF)
+            nc.vector.quantize_mx(
+                out=codes[:, span].bitcast(FP8X4), scales=scales[:, span], in_=src[half][:].rearrange("p n j -> p (n j)")
+            )
+
+        def product(bank, i, codes, scales, t):
+            g, h = TILES[t]
+            part = slice(g * ROWS, (g + 1) * ROWS)
+            nc.tensor.matmul_mx(
+                out=bank[t][:],
+                lhsT=w_words[i][part, 2 * P * h : 2 * P * (h + 1)].bitcast(FP4X4),
+                lhsT_scale=w_scales[part, i * M + P * h : i * M + P * (h + 1)],
+                rhs=codes[part, :].bitcast(FP8X4),
+                rhs_scale=scales[part, :],
+                start=True,
+                stop=True,
+            )
+
+        def const(i, t):
+            g, h = TILES[t]
+            c = i * P + 32 * (2 * g + h)
+            return cols[:, c : c + 1]
+
+        def hbm_rows(a, t):
+            g, h = TILES[t]
+            return a[g, h * P : (h + 1) * P, :]
+
+        def copy_z1(t):
+            nc.scalar.copy(out=z1_sb[t][:], in_=bank_a[t][:])
+
+        def row_mean(t):
+            nc.vector.scalar_tensor_tensor(
+                out=junk_mu[t][:], in0=bank_b[t][:], scalar=1.0 / N, in1=z1_sb[t][:], op0=ALU.mult, op1=ALU.mult, accum_out=mu[t][:]
+            )
+
+        def gate(t):
+            nc.scalar.activation(out=gt[t][:], in_=mu[t][:], func=ACT.Sigmoid, bias=const(1, t), scale=const(0, t))
+            nc.gpsimd.tensor_scalar(out=rest[t][:], in0=gt[t][:], scalar1=-1.0 / N, scalar2=1.0 / N, op0=ALU.mult, op1=ALU.add)
+            nc.gpsimd.tensor_scalar(out=slope[t][:], in0=rest[t][:], scalar1=gt[t][:], scalar2=const(0, t), op0=ALU.mult, op1=ALU.mult)
+
+        def gated(t):
+            nc.scalar.activation(out=u_sb[t][:], in_=bank_a[t][:], func=ACT.Copy, scale=gt[t][:])
+
+        def add_old(t):
+            nc.gpsimd.tensor_tensor(out=v_sb[t][:], in0=u_sb[t][:], in1=old_sb[t][:], op=ALU.add)
+
+        def row_grad(t):
+            nc.vector.scalar_tensor_tensor(
+                out=junk_dg[t][:], in0=bank_a[t][:], scalar=slope[t][:], in1=z1_sb[t][:], op0=ALU.mult, op1=ALU.mult, accum_out=coef[t][:]
+            )
+
+        def finish(t):
+            nc.vector.scalar_tensor_tensor(
+                out=y_sb[t][:], in0=bank_b[t][:], scalar=coef[t][:], in1=v_sb[t][:], op0=ALU.mult, op1=ALU.add
+            )
+            nc.sync.dma_start(out=hbm_rows(out, t), in_=y_sb[t][:])
+
+        nc.vector.memset(w_scales[:].bitcast(I32), 0)
+        nc.vector.memset(rows[:], 0.0)
+        load_scales(nc.scalar, 0, w1_scales)
+        load_half(x_raw, x, 0)
+        load_half(x_raw, x, 1)
+        load_scales(nc.scalar, 1, w2_scales)
+        load_const(0, st)
+        load_const(1, gb)
+        load_scales(nc.gpsimd, 2, wo_scales)
+        load_words(0, w1_words)
+        load_words(1, w2_words)
+        load_half(dy_raw, dy, 0)
+        load_half(dy_raw, dy, 1)
+        load_words(2, wo_words)
+        for t in range(4):
+            nc.sync.dma_start(out=old_sb[t][:], in_=hbm_rows(old, t))
+
+        for half in range(2):
+            cast(nc.vector.tensor_copy, x_bf[half], x_raw[half], 0, V_COLS)
+            cast(nc.scalar.copy, x_bf[half], x_raw[half], V_COLS, HALF)
+            quantize(x_codes, x_scales, x_bf, half)
+        nc.vector.transpose(out=cols[:], in_=rows[:])
+        for pair in range(2):
+            for bank, i in ((bank_a, 0), (bank_b, 1)):
+                for t in (2 * pair, 2 * pair + 1):
+                    product(bank, i, x_codes, x_scales, t)
+
+        cast(nc.vector.tensor_copy, dy_bf[0], dy_raw[0], 0, HALF)
+        quantize(dy_codes, dy_scales, dy_bf, 0)
+        copy_z1(0)
+        copy_z1(1)
+        cast(nc.scalar.copy, dy_bf[1], dy_raw[1], 0, HALF)
+        row_mean(0)
+        row_mean(1)
+        quantize(dy_codes, dy_scales, dy_bf, 1)
+        gate(0)
+        copy_z1(2)
+        gate(1)
+        copy_z1(3)
+        for t in range(4):
+            product(bank_a, 2, dy_codes, dy_scales, t)
+        row_mean(2)
+        row_mean(3)
+        gated(0)
+        gate(2)
+        gated(1)
+        gate(3)
+        gated(2)
+        gated(3)
+        for t in range(4):
+            add_old(t)
+        row_grad(0)
+        for t in range(1, 4):
+            row_grad(t)
+            finish(t - 1)
+        finish(3)

@@ -18,7 +18,9 @@ ACT = mybir.ActivationFunctionType
 P = 128
 ROWS = 64
 HALF = N // 2
-V_COLS = 176
+X_V_COLS = 352
+DY_V_COLS = 384
+LAST_G_COLS = 384
 TILES = [(g, h) for h in range(2) for g in range(G)]
 
 
@@ -34,16 +36,16 @@ def tile_rows_browgate_kernel(tc, x, w1_words, w1_scales, w2_words, w2_scales, s
                 return [pool.tile(shape, dtype, name="%s%d" % (name, i), align_bytes=64) for i in range(count)]
             return [pool.tile(shape, dtype, name="%s%d" % (name, i)) for i in range(count)]
 
-        x_raw = tiles("x_raw", 2, [P, 4, HALF], F32)
-        dy_raw = tiles("dy_raw", 2, [P, 4, HALF], F32)
-        x_bf = tiles("x_bf", 2, [P, HALF, 4], BF16)
-        dy_bf = tiles("dy_bf", 2, [P, HALF, 4], BF16)
+        x_raw, dy_raw = tiles("raw", 2, [P, 4, N], F32)
+        x_bf, dy_bf = tiles("bf", 2, [P, N, 4], BF16)
         x_codes, dy_codes = tiles("codes", 2, [P, N], U32)
         x_scales, dy_scales = tiles("scales", 2, [P, N], U8)
         w_words = tiles("w_words", 3, [P, 2 * M], U8)
         (w_scales,) = tiles("w_scales", 1, [P, 3 * M], U8)
         rows, cols = tiles("consts", 2, [P, 2 * P], F32)
-        old_sb = tiles("old_sb", 4, [P, N], F32)
+        warm_in, warm_out = tiles("warm", 2, [P, 1], F32)
+        old_pair = tiles("old_pair", 2, [P, G, N], F32)
+        old_sb = [old_pair[h][:, g, :] for g, h in TILES]
         z1_sb = tiles("z1_sb", 4, [P, N], F32)
         u_sb = tiles("u_sb", 4, [P, N], F32)
         v_sb = tiles("v_sb", 4, [P, N], F32)
@@ -58,16 +60,15 @@ def tile_rows_browgate_kernel(tc, x, w1_words, w1_scales, w2_words, w2_scales, s
         bank_a = tiles("bank_a", 4, [P, N], F32, ps)
         bank_b = tiles("bank_b", 4, [P, N], F32, ps)
 
-        def load_half(dst, src, half):
-            view = src.rearrange("g (p j) n -> (g p) j n", j=4)
-            nc.sync.dma_start(out=dst[half][:], in_=view[:, :, half * HALF : (half + 1) * HALF])
+        def load_rows(dst, src):
+            nc.sync.dma_start(out=dst[:], in_=src.rearrange("g (p j) n -> (g p) j n", j=4))
 
         def load_words(i, words):
             nc.sync.dma_start(out=w_words[i][:].bitcast(I32), in_=words.rearrange("g p b -> (g p) b").bitcast(I32))
 
-        def load_scales(queue, i, scales):
+        def load_scales(queue, i, scales, quads):
             flat = scales.rearrange("g f m -> (g f) m").bitcast(I32)
-            for q in range(4):
+            for q in quads:
                 queue.dma_start(out=w_scales[32 * q : 32 * q + 4, i * M : (i + 1) * M].bitcast(I32), in_=flat[4 * q : 4 * q + 4, :])
 
         def load_const(i, vec):
@@ -82,11 +83,8 @@ def tile_rows_browgate_kernel(tc, x, w1_words, w1_scales, w2_words, w2_scales, s
                 in_=src[:, :, lo:hi].rearrange("p j (c i) -> p c j i", i=4),
             )
 
-        def quantize(codes, scales, src, half):
-            span = slice(half * HALF, (half + 1) * HALF)
-            nc.vector.quantize_mx(
-                out=codes[:, span].bitcast(FP8X4), scales=scales[:, span], in_=src[half][:].rearrange("p n j -> p (n j)")
-            )
+        def quantize(codes, scales, src):
+            nc.vector.quantize_mx(out=codes[:].bitcast(FP8X4), scales=scales[:], in_=src[:].rearrange("p n j -> p (n j)"))
 
         def product(bank, i, codes, scales, t):
             g, h = TILES[t]
@@ -111,7 +109,7 @@ def tile_rows_browgate_kernel(tc, x, w1_words, w1_scales, w2_words, w2_scales, s
             return a[g, h * P : (h + 1) * P, :]
 
         def copy_z1(t):
-            nc.scalar.copy(out=z1_sb[t][:], in_=bank_a[t][:])
+            nc.scalar.activation(out=z1_sb[t][:], in_=bank_a[t][:], func=ACT.Copy, scale=const(0, t))
 
         def row_mean(t):
             nc.vector.scalar_tensor_tensor(
@@ -119,80 +117,105 @@ def tile_rows_browgate_kernel(tc, x, w1_words, w1_scales, w2_words, w2_scales, s
             )
 
         def gate(t):
-            nc.scalar.activation(out=gt[t][:], in_=mu[t][:], func=ACT.Sigmoid, bias=const(1, t), scale=const(0, t))
+            nc.scalar.activation(out=gt[t][:], in_=mu[t][:], func=ACT.Sigmoid, bias=const(1, t))
+
+        def gate_rest(t):
+            nc.scalar.activation(out=rest[t][:], in_=gt[t][:], func=ACT.Identity, scale=-1.0 / N, bias=1.0 / N)
+
+        def gate_slope(t):
+            nc.scalar.activation(out=slope[t][:], in_=rest[t][:], func=ACT.Copy, scale=gt[t][:])
+
+        def slope_on_gpsimd(t):
             nc.gpsimd.tensor_scalar(out=rest[t][:], in0=gt[t][:], scalar1=-1.0 / N, scalar2=1.0 / N, op0=ALU.mult, op1=ALU.add)
-            nc.gpsimd.tensor_scalar(out=slope[t][:], in0=rest[t][:], scalar1=gt[t][:], scalar2=const(0, t), op0=ALU.mult, op1=ALU.mult)
+            nc.gpsimd.tensor_tensor(out=slope[t][:], in0=rest[t][:], in1=gt[t][:], op=ALU.mult)
 
-        def gated(t):
-            nc.scalar.activation(out=u_sb[t][:], in_=bank_a[t][:], func=ACT.Copy, scale=gt[t][:])
+        def gated_plus_old(t, lo, hi):
+            nc.vector.scalar_tensor_tensor(
+                out=v_sb[t][:, lo:hi], in0=bank_a[t][:, lo:hi], scalar=gt[t][:], in1=old_sb[t][:, lo:hi], op0=ALU.mult, op1=ALU.add
+            )
 
-        def add_old(t):
-            nc.gpsimd.tensor_tensor(out=v_sb[t][:], in0=u_sb[t][:], in1=old_sb[t][:], op=ALU.add)
+        def gated(t, hi):
+            nc.scalar.activation(out=u_sb[t][:, :hi], in_=bank_a[t][:, :hi], func=ACT.Copy, scale=gt[t][:])
+
+        def add_old(t, hi):
+            nc.gpsimd.tensor_tensor(out=v_sb[t][:, :hi], in0=u_sb[t][:, :hi], in1=old_sb[t][:, :hi], op=ALU.add)
 
         def row_grad(t):
             nc.vector.scalar_tensor_tensor(
                 out=junk_dg[t][:], in0=bank_a[t][:], scalar=slope[t][:], in1=z1_sb[t][:], op0=ALU.mult, op1=ALU.mult, accum_out=coef[t][:]
             )
 
-        def finish(t):
+        def finish(t, lo, hi):
             nc.vector.scalar_tensor_tensor(
-                out=y_sb[t][:], in0=bank_b[t][:], scalar=coef[t][:], in1=v_sb[t][:], op0=ALU.mult, op1=ALU.add
+                out=y_sb[t][:, lo:hi], in0=bank_b[t][:, lo:hi], scalar=coef[t][:], in1=v_sb[t][:, lo:hi], op0=ALU.mult, op1=ALU.add
             )
-            nc.sync.dma_start(out=hbm_rows(out, t), in_=y_sb[t][:])
+            nc.sync.dma_start(out=hbm_rows(out, t)[:, lo:hi], in_=y_sb[t][:, lo:hi])
+
+        def cast_shared(dst, src, v_cols):
+            cast(nc.vector.tensor_copy, dst, src, 0, v_cols)
+            cast(nc.scalar.copy, dst, src, v_cols, N)
 
         nc.vector.memset(w_scales[:].bitcast(I32), 0)
-        nc.vector.memset(rows[:], 0.0)
-        load_scales(nc.scalar, 0, w1_scales)
-        load_half(x_raw, x, 0)
-        load_half(x_raw, x, 1)
-        load_scales(nc.scalar, 1, w2_scales)
-        load_const(0, st)
-        load_const(1, gb)
-        load_scales(nc.gpsimd, 2, wo_scales)
+        nc.vector.memset(warm_in[:], 0.0)
+        nc.gpsimd.memset(rows[:], 0.0)
         load_words(0, w1_words)
         load_words(1, w2_words)
-        load_half(dy_raw, dy, 0)
-        load_half(dy_raw, dy, 1)
+        load_rows(x_raw, x)
+        load_scales(nc.scalar, 0, w1_scales, range(4))
+        nc.scalar.activation(out=warm_out[:], in_=warm_in[:], func=ACT.Sigmoid)
+        load_scales(nc.sync, 1, w2_scales, range(2))
+        load_const(0, st)
+        load_const(1, gb)
+        load_scales(nc.gpsimd, 1, w2_scales, range(2, 4))
+        load_rows(dy_raw, dy)
         load_words(2, wo_words)
-        for t in range(4):
-            nc.sync.dma_start(out=old_sb[t][:], in_=hbm_rows(old, t))
+        load_scales(nc.sync, 2, wo_scales, range(4))
+        for h in range(2):
+            nc.sync.dma_start(out=old_pair[h][:], in_=old[:, h * P : (h + 1) * P, :].rearrange("g p n -> p g n"))
 
-        for half in range(2):
-            cast(nc.vector.tensor_copy, x_bf[half], x_raw[half], 0, V_COLS)
-            cast(nc.scalar.copy, x_bf[half], x_raw[half], V_COLS, HALF)
-            quantize(x_codes, x_scales, x_bf, half)
+        cast_shared(x_bf, x_raw, X_V_COLS)
+        quantize(x_codes, x_scales, x_bf)
         nc.vector.transpose(out=cols[:], in_=rows[:])
         for pair in range(2):
             for bank, i in ((bank_a, 0), (bank_b, 1)):
                 for t in (2 * pair, 2 * pair + 1):
                     product(bank, i, x_codes, x_scales, t)
 
-        cast(nc.vector.tensor_copy, dy_bf[0], dy_raw[0], 0, HALF)
-        quantize(dy_codes, dy_scales, dy_bf, 0)
+        cast_shared(dy_bf, dy_raw, DY_V_COLS)
+        quantize(dy_codes, dy_scales, dy_bf)
         copy_z1(0)
         copy_z1(1)
-        cast(nc.scalar.copy, dy_bf[1], dy_raw[1], 0, HALF)
         row_mean(0)
         row_mean(1)
-        quantize(dy_codes, dy_scales, dy_bf, 1)
-        gate(0)
         copy_z1(2)
-        gate(1)
+        gate(0)
         copy_z1(3)
+        gate(1)
         for t in range(4):
             product(bank_a, 2, dy_codes, dy_scales, t)
         row_mean(2)
         row_mean(3)
-        gated(0)
+        slope_on_gpsimd(0)
+        gated(0, N)
+        slope_on_gpsimd(1)
+        add_old(0, N)
         gate(2)
-        gated(1)
+        gated(1, N)
         gate(3)
-        gated(2)
-        gated(3)
-        for t in range(4):
-            add_old(t)
+        gate_rest(2)
+        add_old(1, N)
+        gated(2, N)
+        gate_slope(2)
+        gate_rest(3)
+        add_old(2, N)
+        gated(3, LAST_G_COLS)
+        add_old(3, LAST_G_COLS)
+        gate_slope(3)
         row_grad(0)
         for t in range(1, 4):
             row_grad(t)
-            finish(t - 1)
-        finish(3)
+            if t == 3:
+                gated_plus_old(3, LAST_G_COLS, N)
+            finish(t - 1, 0, N)
+        finish(3, 0, HALF)
+        finish(3, HALF, N)

@@ -166,8 +166,8 @@ def tile_rows_browgate_kernel(tc, x, w1_words, w1_scales, w2_words, w2_scales, s
         load_scales(nc.sync, 1, w2_scales, range(2))
         load_const(0, st)
         load_const(1, gb)
-        load_scales(nc.gpsimd, 1, w2_scales, range(2, 4))
         load_rows(dy_raw, dy)
+        load_scales(nc.sync, 1, w2_scales, range(2, 4))
         load_words(2, wo_words)
         load_scales(nc.sync, 2, wo_scales, range(4))
         for h in range(2):

@@ -16,206 +16,161 @@ ALU = mybir.AluOpType
 ACT = mybir.ActivationFunctionType
 
 P = 128
-ROWS = 64
+PACK = 4
+ROWS = D // PACK
+QUAD = 32
+QUADS = P // QUAD
+SCALE_ROWS = 4
 HALF = N // 2
-X_V_COLS = 352
-DY_V_COLS = 384
-LAST_G_COLS = 384
-TILES = [(g, h) for h in range(2) for g in range(G)]
+VECTOR_COLS = 176
+TILES = [(g, h) for h in range(M // P) for g in range(G)]
+NT = len(TILES)
+W1, W2, WO = range(3)
+ST, GB = range(2)
 
 
 def tile_rows_browgate_kernel(tc, x, w1_words, w1_scales, w2_words, w2_scales, st, gb, wo_words, wo_scales, dy, old, out):
     nc = tc.nc
     with ExitStack() as ctx:
-        sb = ctx.enter_context(tc.tile_pool(name="sb", bufs=1))
-        ps = ctx.enter_context(tc.psum_pool(name="ps", bufs=1))
+        sbuf = ctx.enter_context(tc.tile_pool(name="sbuf", bufs=1))
+        psum = ctx.enter_context(tc.psum_pool(name="psum", bufs=1))
         ctx.enter_context(tc.manual_schedule())
 
-        def tiles(name, count, shape, dtype, pool=sb):
-            if pool is sb:
-                return [pool.tile(shape, dtype, name="%s%d" % (name, i), align_bytes=64) for i in range(count)]
-            return [pool.tile(shape, dtype, name="%s%d" % (name, i)) for i in range(count)]
+        def tiles(name, count, shape, dtype):
+            return [sbuf.tile(shape, dtype, name="%s%d" % (name, i), align_bytes=64) for i in range(count)]
 
-        x_raw, dy_raw = tiles("raw", 2, [P, 4, N], F32)
-        x_bf, dy_bf = tiles("bf", 2, [P, N, 4], BF16)
+        x_raw, dy_raw = tiles("raw", 2, [P, PACK, N], F32)
+        x_bf = tiles("x_bf", 2, [P, HALF, PACK], BF16)
+        dy_bf = tiles("dy_bf", 2, [P, HALF, PACK], BF16)
+        (neg_k,) = tiles("neg_k", 1, [P, NT], F32)
         x_codes, dy_codes = tiles("codes", 2, [P, N], U32)
         x_scales, dy_scales = tiles("scales", 2, [P, N], U8)
         w_words = tiles("w_words", 3, [P, 2 * M], U8)
         (w_scales,) = tiles("w_scales", 1, [P, 3 * M], U8)
-        rows, cols = tiles("consts", 2, [P, 2 * P], F32)
+        vec_rows, vec_cols = tiles("vec", 2, [P, 2 * P], F32)
         warm_in, warm_out = tiles("warm", 2, [P, 1], F32)
-        old_pair = tiles("old_pair", 2, [P, G, N], F32)
-        old_sb = [old_pair[h][:, g, :] for g, h in TILES]
-        z1_sb = tiles("z1_sb", 4, [P, N], F32)
-        u_sb = tiles("u_sb", 4, [P, N], F32)
-        v_sb = tiles("v_sb", 4, [P, N], F32)
-        y_sb = tiles("y_sb", 4, [P, N], F32)
-        junk_mu = tiles("junk_mu", 4, [P, N], F32)
-        junk_dg = tiles("junk_dg", 4, [P, N], F32)
-        mu = tiles("mu", 4, [P, 1], F32)
-        gt = tiles("gt", 4, [P, 1], F32)
-        rest = tiles("rest", 4, [P, 1], F32)
-        slope = tiles("slope", 4, [P, 1], F32)
-        coef = tiles("coef", 4, [P, 1], F32)
-        bank_a = tiles("bank_a", 4, [P, N], F32, ps)
-        bank_b = tiles("bank_b", 4, [P, N], F32, ps)
+        old_half = tiles("old_half", M // P, [P, G, N], F32)
+        zk = tiles("zk", NT, [P, N], F32)
+        gated = tiles("gated", NT - 1, [P, N], F32)
+        partial = tiles("partial", NT, [P, N], F32)
+        result = tiles("result", NT, [P, N], F32)
+        pre_terms = tiles("pre_terms", NT, [P, N], F32)
+        coef_terms = tiles("coef_terms", NT, [P, N], F32)
+        pre = tiles("pre", NT, [P, 1], F32)
+        gt = tiles("gt", NT, [P, 1], F32)
+        slope = tiles("slope", NT, [P, 1], F32)
+        coef = tiles("coef", NT, [P, 1], F32)
+        z1_c0_bank = [psum.tile([P, N], F32, name="z1_c0_bank%d" % t) for t in range(NT)]
+        z2_bank = [psum.tile([P, N], F32, name="z2_bank%d" % t) for t in range(NT)]
 
-        def load_rows(dst, src):
-            nc.sync.dma_start(out=dst[:], in_=src.rearrange("g (p j) n -> (g p) j n", j=4))
+        def load_operand(dst, src):
+            nc.sync.dma_start(out=dst[:], in_=src.rearrange("g (p j) n -> (g p) j n", j=PACK))
 
-        def load_words(i, words):
-            nc.sync.dma_start(out=w_words[i][:].bitcast(I32), in_=words.rearrange("g p b -> (g p) b").bitcast(I32))
+        def load_words(w, words):
+            nc.sync.dma_start(out=w_words[w][:].bitcast(I32), in_=words.rearrange("g p b -> (g p) b").bitcast(I32))
 
-        def load_scales(queue, i, scales, quads):
-            flat = scales.rearrange("g f m -> (g f) m").bitcast(I32)
-            for q in quads:
-                queue.dma_start(out=w_scales[32 * q : 32 * q + 4, i * M : (i + 1) * M].bitcast(I32), in_=flat[4 * q : 4 * q + 4, :])
+        def load_scales(w, scales):
+            rows = scales.rearrange("g b m -> (g b) m").bitcast(I32)
+            for q in range(QUADS):
+                nc.sync.dma_start(
+                    out=w_scales[QUAD * q : QUAD * q + SCALE_ROWS, w * M : (w + 1) * M].bitcast(I32),
+                    in_=rows[SCALE_ROWS * q : SCALE_ROWS * (q + 1), :],
+                )
 
-        def load_const(i, vec):
+        def load_vector(v, vec):
             nc.gpsimd.dma_start(
-                out=rows[0:P:32, i * P : (i + 1) * P].rearrange("a (c j) -> a c j", j=32),
-                in_=vec.rearrange("g (h a j) o -> a (g h) (j o)", a=4, j=32),
+                out=vec_rows[0:P:QUAD, v * P : (v + 1) * P].rearrange("a (c i) -> a c i", i=QUAD),
+                in_=vec.rearrange("g (h a i) o -> a (g h) (i o)", a=QUADS, i=QUAD),
             )
 
-        def cast(copy, dst, src, lo, hi):
+        def round_and_pack(copy, dst, raw, first, lo, hi):
             copy(
                 out=dst[:, lo:hi, :].rearrange("p (c i) j -> p c j i", i=4),
-                in_=src[:, :, lo:hi].rearrange("p j (c i) -> p c j i", i=4),
+                in_=raw[:, :, first + lo : first + hi].rearrange("p j (c i) -> p c j i", i=4),
             )
 
-        def quantize(codes, scales, src):
-            nc.vector.quantize_mx(out=codes[:].bitcast(FP8X4), scales=scales[:], in_=src[:].rearrange("p n j -> p (n j)"))
+        def quantize(codes, scales, halves, raw):
+            for half in range(2):
+                round_and_pack(nc.vector.tensor_copy, halves[half], raw, half * HALF, 0, VECTOR_COLS)
+                round_and_pack(nc.scalar.copy, halves[half], raw, half * HALF, VECTOR_COLS, HALF)
+            for half in range(2):
+                span = slice(half * HALF, (half + 1) * HALF)
+                nc.vector.quantize_mx(
+                    out=codes[:, span].bitcast(FP8X4), scales=scales[:, span], in_=halves[half][:].rearrange("p n j -> p (n j)")
+                )
 
-        def product(bank, i, codes, scales, t):
+        def product(bank, w, codes, scales, t):
             g, h = TILES[t]
             part = slice(g * ROWS, (g + 1) * ROWS)
             nc.tensor.matmul_mx(
                 out=bank[t][:],
-                lhsT=w_words[i][part, 2 * P * h : 2 * P * (h + 1)].bitcast(FP4X4),
-                lhsT_scale=w_scales[part, i * M + P * h : i * M + P * (h + 1)],
+                lhsT=w_words[w][part, 2 * P * h : 2 * P * (h + 1)].bitcast(FP4X4),
+                lhsT_scale=w_scales[part, w * M + P * h : w * M + P * (h + 1)],
                 rhs=codes[part, :].bitcast(FP8X4),
                 rhs_scale=scales[part, :],
                 start=True,
                 stop=True,
             )
 
-        def const(i, t):
-            g, h = TILES[t]
-            c = i * P + 32 * (2 * g + h)
-            return cols[:, c : c + 1]
+        def multiply_add(dst, bank, factor, other, op, total=None):
+            nc.vector.scalar_tensor_tensor(out=dst, in0=bank, scalar=factor, in1=other, op0=ALU.mult, op1=op, accum_out=total)
 
-        def hbm_rows(a, t):
-            g, h = TILES[t]
-            return a[g, h * P : (h + 1) * P, :]
-
-        def copy_z1(t):
-            nc.scalar.activation(out=z1_sb[t][:], in_=bank_a[t][:], func=ACT.Copy, scale=const(0, t))
-
-        def row_mean(t):
-            nc.vector.scalar_tensor_tensor(
-                out=junk_mu[t][:], in0=bank_b[t][:], scalar=1.0 / N, in1=z1_sb[t][:], op0=ALU.mult, op1=ALU.mult, accum_out=mu[t][:]
-            )
-
-        def gate(t):
-            nc.scalar.activation(out=gt[t][:], in_=mu[t][:], func=ACT.Sigmoid, bias=const(1, t))
-
-        def gate_rest(t):
-            nc.scalar.activation(out=rest[t][:], in_=gt[t][:], func=ACT.Identity, scale=-1.0 / N, bias=1.0 / N)
-
-        def gate_slope(t):
-            nc.scalar.activation(out=slope[t][:], in_=rest[t][:], func=ACT.Copy, scale=gt[t][:])
-
-        def slope_on_gpsimd(t):
-            nc.gpsimd.tensor_scalar(out=rest[t][:], in0=gt[t][:], scalar1=-1.0 / N, scalar2=1.0 / N, op0=ALU.mult, op1=ALU.add)
-            nc.gpsimd.tensor_tensor(out=slope[t][:], in0=rest[t][:], in1=gt[t][:], op=ALU.mult)
-
-        def gated_plus_old(t, lo, hi):
-            nc.vector.scalar_tensor_tensor(
-                out=v_sb[t][:, lo:hi], in0=bank_a[t][:, lo:hi], scalar=gt[t][:], in1=old_sb[t][:, lo:hi], op0=ALU.mult, op1=ALU.add
-            )
-
-        def gated(t, hi):
-            nc.scalar.activation(out=u_sb[t][:, :hi], in_=bank_a[t][:, :hi], func=ACT.Copy, scale=gt[t][:])
-
-        def add_old(t, hi):
-            nc.gpsimd.tensor_tensor(out=v_sb[t][:, :hi], in0=u_sb[t][:, :hi], in1=old_sb[t][:, :hi], op=ALU.add)
-
-        def row_grad(t):
-            nc.vector.scalar_tensor_tensor(
-                out=junk_dg[t][:], in0=bank_a[t][:], scalar=slope[t][:], in1=z1_sb[t][:], op0=ALU.mult, op1=ALU.mult, accum_out=coef[t][:]
-            )
+        def row_coef(t):
+            multiply_add(coef_terms[t][:], z1_c0_bank[t][:], slope[t][:], zk[t][:], ALU.mult, coef[t][:])
 
         def finish(t, lo, hi):
-            nc.vector.scalar_tensor_tensor(
-                out=y_sb[t][:, lo:hi], in0=bank_b[t][:, lo:hi], scalar=coef[t][:], in1=v_sb[t][:, lo:hi], op0=ALU.mult, op1=ALU.add
-            )
-            nc.sync.dma_start(out=hbm_rows(out, t)[:, lo:hi], in_=y_sb[t][:, lo:hi])
-
-        def cast_shared(dst, src, v_cols):
-            cast(nc.vector.tensor_copy, dst, src, 0, v_cols)
-            cast(nc.scalar.copy, dst, src, v_cols, N)
+            g, h = TILES[t]
+            multiply_add(result[t][:, lo:hi], z2_bank[t][:, lo:hi], coef[t][:], partial[t][:, lo:hi], ALU.add)
+            nc.sync.dma_start(out=out[g, h * P : (h + 1) * P, lo:hi], in_=result[t][:, lo:hi])
 
         nc.vector.memset(w_scales[:].bitcast(I32), 0)
         nc.vector.memset(warm_in[:], 0.0)
-        nc.gpsimd.memset(rows[:], 0.0)
-        load_words(0, w1_words)
-        load_words(1, w2_words)
-        load_rows(x_raw, x)
-        load_scales(nc.scalar, 0, w1_scales, range(4))
+        nc.gpsimd.memset(vec_rows[:], 0.0)
+
+        load_operand(x_raw, x)
+        load_words(W1, w1_words)
+        load_words(W2, w2_words)
+        load_scales(W1, w1_scales)
+        load_operand(dy_raw, dy)
         nc.scalar.activation(out=warm_out[:], in_=warm_in[:], func=ACT.Sigmoid)
-        load_scales(nc.sync, 1, w2_scales, range(2))
-        load_const(0, st)
-        load_const(1, gb)
-        load_rows(dy_raw, dy)
-        load_scales(nc.sync, 1, w2_scales, range(2, 4))
-        load_words(2, wo_words)
-        load_scales(nc.sync, 2, wo_scales, range(4))
-        for h in range(2):
-            nc.sync.dma_start(out=old_pair[h][:], in_=old[:, h * P : (h + 1) * P, :].rearrange("g p n -> p g n"))
+        load_vector(ST, st)
+        load_vector(GB, gb)
+        load_scales(W2, w2_scales)
+        load_words(WO, wo_words)
+        load_scales(WO, wo_scales)
+        for h in range(M // P):
+            nc.sync.dma_start(out=old_half[h][:], in_=old[:, h * P : (h + 1) * P, :].rearrange("g p n -> p g n"))
 
-        cast_shared(x_bf, x_raw, X_V_COLS)
-        quantize(x_codes, x_scales, x_bf)
-        nc.vector.transpose(out=cols[:], in_=rows[:])
-        for pair in range(2):
-            for bank, i in ((bank_a, 0), (bank_b, 1)):
-                for t in (2 * pair, 2 * pair + 1):
-                    product(bank, i, x_codes, x_scales, t)
+        quantize(x_codes, x_scales, x_bf, x_raw)
+        nc.vector.transpose(out=vec_cols[:], in_=vec_rows[:])
+        nc.gpsimd.tensor_scalar(
+            out=neg_k[:], in0=vec_cols[:, ST * P : (ST + 1) * P : QUAD], scalar1=-1.0 / N, scalar2=0.0, op0=ALU.mult, op1=ALU.add
+        )
+        for bank, w in ((z1_c0_bank, W1), (z2_bank, W2)):
+            for t in range(NT):
+                product(bank, w, x_codes, x_scales, t)
+        quantize(dy_codes, dy_scales, dy_bf, dy_raw)
 
-        cast_shared(dy_bf, dy_raw, DY_V_COLS)
-        quantize(dy_codes, dy_scales, dy_bf)
-        copy_z1(0)
-        copy_z1(1)
-        row_mean(0)
-        row_mean(1)
-        copy_z1(2)
-        gate(0)
-        copy_z1(3)
-        gate(1)
-        for t in range(4):
-            product(bank_a, 2, dy_codes, dy_scales, t)
-        row_mean(2)
-        row_mean(3)
-        slope_on_gpsimd(0)
-        gated(0, N)
-        slope_on_gpsimd(1)
-        add_old(0, N)
-        gate(2)
-        gated(1, N)
-        gate(3)
-        gate_rest(2)
-        add_old(1, N)
-        gated(2, N)
-        gate_slope(2)
-        gate_rest(3)
-        add_old(2, N)
-        gated(3, LAST_G_COLS)
-        add_old(3, LAST_G_COLS)
-        gate_slope(3)
-        row_grad(0)
-        for t in range(1, 4):
-            row_grad(t)
-            if t == 3:
-                gated_plus_old(3, LAST_G_COLS, N)
+        for t, (g, h) in enumerate(TILES):
+            c = (M // P) * g + h
+            nc.scalar.activation(out=zk[t][:], in_=z1_c0_bank[t][:], func=ACT.Copy, scale=neg_k[:, c : c + 1])
+            multiply_add(pre_terms[t][:], z2_bank[t][:], -1.0, zk[t][:], ALU.mult, pre[t][:])
+
+        for t, (g, h) in enumerate(TILES):
+            gb_col = GB * P + QUAD * ((M // P) * g + h)
+            product(z1_c0_bank, WO, dy_codes, dy_scales, t)
+            nc.scalar.activation(out=gt[t][:], in_=pre[t][:], func=ACT.Sigmoid, bias=vec_cols[:, gb_col : gb_col + 1])
+            nc.gpsimd.tensor_scalar(out=slope[t][:], in0=gt[t][:], scalar1=-1.0, scalar2=gt[t][:], op0=ALU.add, op1=ALU.mult)
+
+        for t, (g, h) in list(enumerate(TILES))[1:]:
+            nc.scalar.activation(out=gated[t - 1][:], in_=z1_c0_bank[t][:], func=ACT.Copy, scale=gt[t][:])
+            nc.gpsimd.tensor_tensor(out=partial[t][:], in0=gated[t - 1][:], in1=old_half[h][:, g, :], op=ALU.add)
+
+        g, h = TILES[0]
+        row_coef(0)
+        multiply_add(partial[0][:], z1_c0_bank[0][:], gt[0][:], old_half[h][:, g, :], ALU.add)
+        for t in range(1, NT):
+            row_coef(t)
             finish(t - 1, 0, N)
-        finish(3, 0, HALF)
-        finish(3, HALF, N)
+        finish(NT - 1, 0, HALF)
+        finish(NT - 1, HALF, N)

from contextlib import ExitStack

import concourse.mybir as mybir

G, D, M, N = 2, 256, 256, 512
FLOPS = 3 * 2 * G * D * M * N

F32 = mybir.dt.float32
BF16 = mybir.dt.bfloat16
I32 = mybir.dt.int32
U32 = mybir.dt.uint32
U8 = mybir.dt.uint8
FP8X4 = mybir.dt.float8_e4m3fn_x4
FP4X4 = mybir.dt.float4_e2m1fn_x4
ALU = mybir.AluOpType
ACT = mybir.ActivationFunctionType

P = 128
PACK = 4
ROWS = D // PACK
QUAD = 32
QUADS = P // QUAD
SCALE_ROWS = 4
HALF = N // 2
VECTOR_COLS = 176
TILES = [(g, h) for h in range(M // P) for g in range(G)]
NT = len(TILES)
W1, W2, WO = range(3)
ST, GB = range(2)


def tile_rows_browgate_kernel(tc, x, w1_words, w1_scales, w2_words, w2_scales, st, gb, wo_words, wo_scales, dy, old, out):
    nc = tc.nc
    with ExitStack() as ctx:
        sbuf = ctx.enter_context(tc.tile_pool(name="sbuf", bufs=1))
        psum = ctx.enter_context(tc.psum_pool(name="psum", bufs=1))
        ctx.enter_context(tc.manual_schedule())

        def tiles(name, count, shape, dtype):
            return [sbuf.tile(shape, dtype, name="%s%d" % (name, i), align_bytes=64) for i in range(count)]

        x_raw, dy_raw = tiles("raw", 2, [P, PACK, N], F32)
        x_bf = tiles("x_bf", 2, [P, HALF, PACK], BF16)
        dy_bf = tiles("dy_bf", 2, [P, HALF, PACK], BF16)
        (neg_k,) = tiles("neg_k", 1, [P, NT], F32)
        x_codes, dy_codes = tiles("codes", 2, [P, N], U32)
        x_scales, dy_scales = tiles("scales", 2, [P, N], U8)
        w_words = tiles("w_words", 3, [P, 2 * M], U8)
        (w_scales,) = tiles("w_scales", 1, [P, 3 * M], U8)
        vec_rows, vec_cols = tiles("vec", 2, [P, 2 * P], F32)
        warm_in, warm_out = tiles("warm", 2, [P, 1], F32)
        old_half = tiles("old_half", M // P, [P, G, N], F32)
        zk = tiles("zk", NT, [P, N], F32)
        gated = tiles("gated", NT - 1, [P, N], F32)
        partial = tiles("partial", NT, [P, N], F32)
        result = tiles("result", NT, [P, N], F32)
        pre_terms = tiles("pre_terms", NT, [P, N], F32)
        coef_terms = tiles("coef_terms", NT, [P, N], F32)
        pre = tiles("pre", NT, [P, 1], F32)
        gt = tiles("gt", NT, [P, 1], F32)
        slope = tiles("slope", NT, [P, 1], F32)
        coef = tiles("coef", NT, [P, 1], F32)
        z1_c0_bank = [psum.tile([P, N], F32, name="z1_c0_bank%d" % t) for t in range(NT)]
        z2_bank = [psum.tile([P, N], F32, name="z2_bank%d" % t) for t in range(NT)]

        def load_operand(dst, src):
            nc.sync.dma_start(out=dst[:], in_=src.rearrange("g (p j) n -> (g p) j n", j=PACK))

        def load_words(w, words):
            nc.sync.dma_start(out=w_words[w][:].bitcast(I32), in_=words.rearrange("g p b -> (g p) b").bitcast(I32))

        def load_scales(w, scales):
            rows = scales.rearrange("g b m -> (g b) m").bitcast(I32)
            for q in range(QUADS):
                nc.sync.dma_start(
                    out=w_scales[QUAD * q : QUAD * q + SCALE_ROWS, w * M : (w + 1) * M].bitcast(I32),
                    in_=rows[SCALE_ROWS * q : SCALE_ROWS * (q + 1), :],
                )

        def load_vector(v, vec):
            nc.gpsimd.dma_start(
                out=vec_rows[0:P:QUAD, v * P : (v + 1) * P].rearrange("a (c i) -> a c i", i=QUAD),
                in_=vec.rearrange("g (h a i) o -> a (g h) (i o)", a=QUADS, i=QUAD),
            )

        def round_and_pack(copy, dst, raw, first, lo, hi):
            copy(
                out=dst[:, lo:hi, :].rearrange("p (c i) j -> p c j i", i=4),
                in_=raw[:, :, first + lo : first + hi].rearrange("p j (c i) -> p c j i", i=4),
            )

        def quantize(codes, scales, halves, raw):
            for half in range(2):
                round_and_pack(nc.vector.tensor_copy, halves[half], raw, half * HALF, 0, VECTOR_COLS)
                round_and_pack(nc.scalar.copy, halves[half], raw, half * HALF, VECTOR_COLS, HALF)
            for half in range(2):
                span = slice(half * HALF, (half + 1) * HALF)
                nc.vector.quantize_mx(
                    out=codes[:, span].bitcast(FP8X4), scales=scales[:, span], in_=halves[half][:].rearrange("p n j -> p (n j)")
                )

        def product(bank, w, codes, scales, t):
            g, h = TILES[t]
            part = slice(g * ROWS, (g + 1) * ROWS)
            nc.tensor.matmul_mx(
                out=bank[t][:],
                lhsT=w_words[w][part, 2 * P * h : 2 * P * (h + 1)].bitcast(FP4X4),
                lhsT_scale=w_scales[part, w * M + P * h : w * M + P * (h + 1)],
                rhs=codes[part, :].bitcast(FP8X4),
                rhs_scale=scales[part, :],
                start=True,
                stop=True,
            )

        def multiply_add(dst, bank, factor, other, op, total=None):
            nc.vector.scalar_tensor_tensor(out=dst, in0=bank, scalar=factor, in1=other, op0=ALU.mult, op1=op, accum_out=total)

        def row_coef(t):
            multiply_add(coef_terms[t][:], z1_c0_bank[t][:], slope[t][:], zk[t][:], ALU.mult, coef[t][:])

        def finish(t, lo, hi):
            g, h = TILES[t]
            multiply_add(result[t][:, lo:hi], z2_bank[t][:, lo:hi], coef[t][:], partial[t][:, lo:hi], ALU.add)
            nc.sync.dma_start(out=out[g, h * P : (h + 1) * P, lo:hi], in_=result[t][:, lo:hi])

        nc.vector.memset(w_scales[:].bitcast(I32), 0)
        nc.vector.memset(warm_in[:], 0.0)
        nc.gpsimd.memset(vec_rows[:], 0.0)

        load_operand(x_raw, x)
        load_words(W1, w1_words)
        load_words(W2, w2_words)
        load_scales(W1, w1_scales)
        load_operand(dy_raw, dy)
        nc.scalar.activation(out=warm_out[:], in_=warm_in[:], func=ACT.Sigmoid)
        load_vector(ST, st)
        load_vector(GB, gb)
        load_scales(W2, w2_scales)
        load_words(WO, wo_words)
        load_scales(WO, wo_scales)
        for h in range(M // P):
            nc.sync.dma_start(out=old_half[h][:], in_=old[:, h * P : (h + 1) * P, :].rearrange("g p n -> p g n"))

        quantize(x_codes, x_scales, x_bf, x_raw)
        nc.vector.transpose(out=vec_cols[:], in_=vec_rows[:])
        nc.gpsimd.tensor_scalar(
            out=neg_k[:], in0=vec_cols[:, ST * P : (ST + 1) * P : QUAD], scalar1=-1.0 / N, scalar2=0.0, op0=ALU.mult, op1=ALU.add
        )
        for bank, w in ((z1_c0_bank, W1), (z2_bank, W2)):
            for t in range(NT):
                product(bank, w, x_codes, x_scales, t)
        quantize(dy_codes, dy_scales, dy_bf, dy_raw)

        for t, (g, h) in enumerate(TILES):
            c = (M // P) * g + h
            nc.scalar.activation(out=zk[t][:], in_=z1_c0_bank[t][:], func=ACT.Copy, scale=neg_k[:, c : c + 1])
            multiply_add(pre_terms[t][:], z2_bank[t][:], -1.0, zk[t][:], ALU.mult, pre[t][:])

        for t, (g, h) in enumerate(TILES):
            gb_col = GB * P + QUAD * ((M // P) * g + h)
            product(z1_c0_bank, WO, dy_codes, dy_scales, t)
            nc.scalar.activation(out=gt[t][:], in_=pre[t][:], func=ACT.Sigmoid, bias=vec_cols[:, gb_col : gb_col + 1])
            nc.gpsimd.tensor_scalar(out=slope[t][:], in0=gt[t][:], scalar1=-1.0, scalar2=gt[t][:], op0=ALU.add, op1=ALU.mult)

        for t, (g, h) in list(enumerate(TILES))[1:]:
            nc.scalar.activation(out=gated[t - 1][:], in_=z1_c0_bank[t][:], func=ACT.Copy, scale=gt[t][:])
            nc.gpsimd.tensor_tensor(out=partial[t][:], in0=gated[t - 1][:], in1=old_half[h][:, g, :], op=ALU.add)

        g, h = TILES[0]
        row_coef(0)
        multiply_add(partial[0][:], z1_c0_bank[0][:], gt[0][:], old_half[h][:, g, :], ALU.add)
        for t in range(1, NT):
            row_coef(t)
            finish(t - 1, 0, N)
        finish(NT - 1, 0, HALF)
        finish(NT - 1, HALF, N)
